import numpy as np, ml_dtypes
CORES = [16,18,20,22]
N = 4
BF = ml_dtypes.bfloat16
def gentries(a):
    return np.ascontiguousarray(a.reshape(8, 16, -1).transpose(0, 2, 1)).reshape(8, -1)
def gtable(e):
    e = np.asarray(e); return np.ascontiguousarray(e.reshape(8, -1, 16).transpose(0, 2, 1)).reshape(128, -1).astype(np.int32)
L, CAP, S, RO, PA = 1280, 256, 128, 3, 2
V = L + RO * CAP; W = V + (N - 1) * 2 * S + 1; NONE = W - 1
G8 = np.arange(8)[:, None]
ARR = np.concatenate([V + (d - 1) * 2 * S + np.arange(S) for d in range(1, N)])
def columns(x):
    return np.ascontiguousarray(x.reshape(N, 8, 16, -1).transpose(0, 1, 3, 2))
def flat(x):
    return np.ascontiguousarray(x.transpose(0, 1, 3, 2)).reshape(N, 128, -1)
def slots(rng, n, share):
    e = rng.integers(0, L, (N, 8, L, 16)); far = ARR[rng.integers(0, len(ARR), e.shape)]
    e = np.where(rng.random(e.shape) < share, far, e)
    return np.where(np.argsort(rng.random(e.shape), axis=-1) < n, e, NONE)
def showing(rng):
    return np.ascontiguousarray(np.argsort(rng.random((N, 8, N - 1, L)), axis=-1)[..., :S])
def pack(e, v, th, sh):
    return {"e": flat(e).astype(np.int32), "v0": flat(v).astype(np.float32).astype(BF), "th": np.ascontiguousarray(np.repeat(th, 16, axis=1)[:, :, None]).astype(np.int32),
            "sh": np.stack([gtable(a.reshape(8, -1)) for a in sh])}
def setup_inputs(rng):
    e = slots(rng, rng.integers(6, 17, (N, 8, L, 1)), 0.3)
    v = (256 * (0.25 + 0.75 * rng.random((N, 8, L, 1))) * rng.random((N, 8, L, 16))).astype(np.int64)
    base = np.array([120, 250, 400, 550, 700, 900, 1100, 1400])
    th = base[np.argsort(rng.random((N, 8)), axis=1)] + rng.integers(-50, 51, (N, 8))
    return pack(e, v, th, showing(rng))
def setup_inputs_room(rng):
    e = slots(rng, rng.integers(15, 17, (N, 8, L, 1)), 0.3)
    n = rng.choice(np.array([0, 1, CAP - 1, CAP, CAP + 1, L]), (N, 8)); n[0] = [CAP, CAP + 1, L, CAP - 1, 1, 0, CAP, CAP + 1]
    hot = np.argsort(rng.random((N, 8, L)), axis=-1) < n[:, :, None]; hot[0, 4] = False; hot[0, 4, L - 1] = True
    v = np.where(hot[..., None], rng.integers(200, 256, (N, 8, L, 16)), rng.integers(136, 200, (N, 8, L, 16)))
    return pack(e, v, np.full((N, 8), 3200), showing(rng))
def setup_inputs_ties(rng):
    e = slots(rng, rng.choice(np.array([8, 10, 12, 16]), (N, 8, L, 1)), 0.3)
    base = rng.integers(8, 128, (1, 8, 1, 16)); kind = rng.integers(1, 3, (N, 8, L, 1)); kind[:, ::2] = 2
    add = rng.integers(0, 2, (N, 8)); add[0] = 0; add[1, ::2] = 1
    th = np.sum(base, axis=-1)[..., 0] * np.where(np.arange(8) % 2 == 0, 2, 1)[None, :] + add
    return pack(e, base * kind, th, showing(rng))
def setup_inputs_ends(rng):
    e = slots(rng, rng.integers(10, 17, (N, 8, L, 1)), 0.3); v = rng.integers(60, 256, (N, 8, L, 16)); sh = showing(rng)
    e[:, 0] = rng.choice(np.array([0, L - 1, L, V - 1, V, V + S - 1, V + S, W - 2, NONE]), (N, L, 16))
    e[:, 1] = rng.integers(0, W, (N, L, 16)); e[:, 2] = ARR[rng.integers(0, len(ARR), (N, L, 16))]; e[:, 3] = rng.integers(0, L, (N, L, 16))
    e[:, 4] = rng.integers(0, L, (N, L, 1)); e[:, 4, :, 9] = NONE
    e[:, 5] = np.where(rng.random((N, L, 1)) < 0.3, NONE, e[:, 5])
    sh[:, ::2] = rng.choice(np.array([0, L - 1, L >> 1, 3]), (N, 4, N - 1, S))
    th = rng.choice(np.array([1, 2, 500, 1500]), (N, 8)); th[0, 7] = 4096; th[1, 0] = 1
    return pack(e, v, th, sh)
def setup_inputs_heavy(rng):
    e = slots(rng, rng.integers(0, 4, (N, 8, L, 1)), 0.2); v = rng.integers(1, 32, (N, 8, L, 16))
    o = 8 + np.argsort(rng.random((N, 8, L - 8)), axis=-1)[..., :64]; kind = rng.integers(0, 4, (N, 8, L))
    a = np.take_along_axis(o, rng.integers(0, 64, (N, 8, L)), 2); b = np.take_along_axis(o, rng.integers(0, 64, (N, 8, L)), 2)
    e[..., 0] = np.where((kind == 0) | (kind == 3), a, e[..., 0]); e[..., 15] = np.where((kind == 1) | (kind == 3), b, e[..., 15])
    one = np.arange(16) == rng.integers(0, 16, (N, 8, L, 1))
    e = np.where(kind[..., None] == 2, np.where(one, a[..., None], NONE), e)
    for q in range(N):
        for g in range(8):
            e[q, g, o[q, g]] = rng.choice(o[q, g], (64, 16)); v[q, g, o[q, g]] = 255
    e[:, :, 0] = NONE; v[:, :, :PA + 1] = 200
    for j in range(1, PA + 1): e[:, :, j] = j - 1
    e[:, ::2, PA, 0] = NONE
    th = rng.choice(np.array([1, 150, 250, 4080]), (N, 8)); th[0, 0] = 150; th[1, 3] = 4080; th[2, 5] = 2040; th[3, 3] = 4081; th[:, 6:] = 1
    sh = showing(rng)
    e[:, 6, :, 8:] = np.arange(L)[None, :, None]; v[:, 6] = rng.integers(1, 256, (N, L, 16))
    at = 0
    for r in range(RO):
        m = at + PA * (r + 1); e[:, 6, at] = NONE; v[:, 6, at:m + 1] = 200
        for j in range(at + 1, m + 1): e[:, 6, j] = j - 1
        e[1::2, 6, m, 0] = NONE
        at = m + 1 + CAP
    e[:, 6, PA + 1] = PA + 3; e[:, 6, PA + 1, 0] = PA + 2; v[:, 6, PA + 2] = 250; v[:, 6, PA + 3] = 255
    v[:, 6, L - 16:] = 0; e[:, 6, L - 16:] = NONE; e[:, 6, L - 16:, 3] = PA + 4; e[:, 6, L - 32:L - 16, 5] = np.arange(L - 16, L)
    t0 = (RO - 1) * CAP + 1; pool = np.concatenate([t0 + np.arange(CAP - 1), ARR])
    e[:, 7] = pool[rng.integers(0, len(pool), (N, L, 16))]; e[:, 7, :, 5:11] = NONE
    v[:, 7] = rng.integers(1, 256, (N, L, 16)); v[:, 7, t0:t0 + CAP - 1] = rng.integers(204, 256, (N, CAP - 1, 16))
    sh[:, 7] = t0 + np.argsort(rng.random((N, N - 1, CAP - 1)), axis=-1)[..., :S]; sh[:, 7, 0] = t0 + rng.integers(0, CAP - 1, (N, 1))
    e[:, 7, 0, 0] = ARR[-1]; e[:, 7, 1, 0] = V + S - 1
    e[1, 7, L - 1] = NONE; v[1, 7, L - 1] = 255; sh[1, 7, 1, 0] = L - 1; e[3, 7, 2] = V + 2 * S; v[3, 7, 2] = 255
    return pack(e, v, th, sh)
def setup_inputs_spread(rng):
    e = slots(rng, 16 - (14 * rng.random((N, 8, L, 1)) ** 2).astype(np.int64), 0.3)
    e = np.where((e < L) & (rng.random(e.shape) < 0.7), (L * rng.random(e.shape) ** 3).astype(np.int64), e)
    v = np.minimum((np.exp2(3 + 5 * rng.random((N, 8, L, 1))) * rng.random((N, 8, L, 16))).astype(np.int64), 255)
    th = np.minimum(np.maximum(np.exp2(12 * rng.random((N, 8))).astype(np.int64), 1), 4096); th[:, 2] = np.minimum(th[:, 2], 30)
    return pack(e, v, th, showing(rng))
def check_inputs(d):
    bad = []
    for k, lo, hi in (("e", 0, W - 1), ("th", 1, 4096), ("sh", 0, L - 1)):
        if np.min(d[k]) < lo or np.max(d[k]) > hi: bad.append("range of " + k)
    x = np.asarray(d["v0"]).astype(np.float64)
    if not np.all((x >= 0) & (x <= 255) & (x == np.floor(x))): bad.append("v0 is not whole numbers from 0 to 255")
    t = np.asarray(d["th"]).reshape(N, 8, 16)
    if not np.all(t == t[:, :, :1]): bad.append("th differs inside a group")
    return bad
def reference(e, v0, th, sh):
    E = np.full((N, 8, V, 16), NONE, np.int32); E[:, :, :L] = columns(e)
    v = np.zeros((N, 8, V, 16), np.int32); v[:, :, :L] = columns(v0.astype(np.float32)).astype(np.int32)
    t = th.reshape(N, 8, 16)[:, :, 0].astype(np.int64)
    half = np.full((N, 8, L), V, np.int64)
    sl = np.stack([gentries(a) for a in sh]).astype(np.int64).reshape(N, 8, N - 1, S)
    def show():
        z = np.concatenate([v, np.zeros((N, 8, 1, 16), np.int32)], axis=2); w = np.zeros((N, 8, W, 16), np.int32); w[:, :, :V] = v
        for a in range(N):
            for d in range(1, N):
                q = (a - d) % N; ix = sl[q, :, d - 1]; b = V + (d - 1) * 2 * S
                w[a, :, b:b + S] = z[q][G8, ix]; w[a, :, b + S:b + 2 * S] = z[q][G8, half[q][G8, ix]]
        return w
    for rnd in range(RO):
        for step in range(PA):
            w = show()
            for a in range(N):
                for g in range(8):
                    v[a, g] = np.minimum(v[a, g], np.add.reduce(w[a, g][E[a, g]], axis=1) >> 3)
        w = show(); fresh = np.zeros((N, 8, L), bool); new = np.full((N, 8, W), -1, np.int32)
        for a in range(N):
            for g in range(8):
                s = np.flatnonzero((half[a, g] == V) & (np.add.reduce(v[a, g, :L], axis=1) >= t[a, g]))[:CAP]
                h = L + CAP * rnd + np.arange(len(s)); old = E[a, g, s]
                C = np.add.accumulate(np.add.reduce(w[a, g][old], axis=2), axis=1)
                cut = np.argmax(2 * C >= C[:, 15:], axis=1); behind = np.arange(16)[None, :] > cut[:, None]
                E[a, g, h] = np.where(behind, old, NONE); E[a, g, s] = np.where(behind, NONE, old)
                x = (v[a, g, s] + 1) >> 1; v[a, g, s] = x; v[a, g, h] = x
                half[a, g, s] = h; fresh[a, g, s] = True; new[a, g, s] = h
        for a in range(N):
            for d in range(1, N):
                q = (a - d) % N; ix = sl[q, :, d - 1]; b = V + (d - 1) * 2 * S
                new[a, :, b:b + S] = np.where(fresh[q][G8, ix], b + S + np.arange(S)[None, :], -1)
            for g in range(8):
                n = new[a, g][E[a, g]]; has = n >= 0; empty = E[a, g] == NONE
                i = np.argmax(has, axis=1); m = np.argmax(empty, axis=1); c = np.flatnonzero(np.any(has, axis=1) & np.any(empty, axis=1))
                E[a, g, c, m[c]] = n[c, i[c]]
    return {"ye": flat(E).astype(np.float32), "yv": flat(v).astype(np.float32).astype(BF)}

from concourse.bass import DstId, RemoteDMATransfer
from concourse.mybir import AluOpType as OP, ActivationFunctionType as AF

N, L, CAP, RO, NV, W = 4, 1280, 256, 3, 2048, 2817
NONE, K = 2816, 1792
M = 12582912.0
NGB = 16
PARTS = ((0, 64), (64, 80))
ONLY_S = (896, 1024, 1408)
PIECE, SUB = 128, 64

BF, F32, F16, U16, I32 = "bfloat16", "float32", "float16", "uint16", "int32"
_S = {
    "e32": (1280, I32), "v016": (1280, BF), "thi": (1, I32), "thf": (1, F32), "shi": (24, I32), "shl": (24, U16), "SH": (48, U16),
    "A": (2824, F32), "B": (2824, F32), "VF": (2832, BF), "E": (2048, F32), "Lu": (2048, U16), "H": (2824, F32),
    "ONE": (2048, BF), "BD": (2048, BF), "Rm": (2048, BF), "Dm": (2048, BF), "Wt": (2048, BF), "Ls": (2048, BF), "R16": (2048, F16),
    "Id": (128, BF), "Id8": (128, BF), "Ihi": (128, BF), "Ilo": (128, BF), "dneg": (128, BF), "dmag": (128, BF), "dsp": (128, BF), "BO32": (128, BF),
    "TRI": (128, BF), "PXl": (128, BF), "U1": (128, BF), "U2": (128, BF),
    "ki": (1, I32), "ka": (1, I32), "km": (1, F32), "thr": (1, F32), "c1": (1, F32), "c2": (1, F32), "cc": (1, F32), "mhi": (1, F32), "mlo": (1, F32),
    "pc": (3, F32), "ini": (1, F32), "d16": (80, F32), "DU0": (80, F32), "DU": (80, F32), "CH": (1280, BF), "CL": (1280, BF), "CI": (1280, BF), "HJ": (768, F32),
    "cand": (80, BF), "SC": (80, F32), "pd": (80, F32), "tt": (80, F32), "of": (80, F32), "ofu": (80, U16), "val": (80, BF), "spl": (80, BF),
    "SLW": (2560, BF), "SL": (16, U16), "EO": (256, F32), "XS": (256, F32), "NB": (256, F32), "FN": (256, BF), "HG": (384, F16), "EL": (256, U16),
    "TO": (256, F32), "BH": (256, BF), "TB": (256, F32), "ES": (256, F32), "SND": (768, F32), "SNDh": (768, BF),
    "em": (2048, BF), "fe": (2048, BF), "fl": (2048, BF), "prod": (2048, F16), "tl": (128, U16), "fp": (2048, F32), "xp": (1792, BF), "xi": (1792, BF),
    "YV": (2048, BF),
}
for _k in range(NGB):
    _S["gb%d" % _k] = (2048, BF)
SCRATCH = {k: ("sbuf", [128, n], t) for k, (n, t) in _S.items()}
for _k in range(8):
    SCRATCH["p%d" % _k] = ("psum", [128, 512], "float32")
NSTEP = 3 * RO + 1
SEMAPHORES = ["qv", "qs", "qt", "qg"] + ["arr%d" % k for k in range(NSTEP)] + ["snd%d" % k for k in range(NSTEP)] + ["d%d" % k for k in range(24)]

CYC, GAT, SCA, PEC = 1.04, 1.62, 3.9, 0.52
WAKE, OWN = 130.0, 60.0
NET, DMA = 3500.0, 2300.0
BOOST = 40000.0


def bank(buf):
    return len(buf) == 2 and buf[0] == "p" and buf[1].isdigit()


def add(P, q, fn, outs, ins, cost, token=None, lat=0.0, after=(), boost=0.0):
    ops, acc = P["ops"], P["acc"]
    me = len(ops)
    deps = {a: True for a in after}
    for lst, w in ((ins, False), (outs, True)):
        for buf, lo, hi in lst:
            recs = acc.setdefault(buf, [])
            if bank(buf):
                for ro in recs:
                    if ro != me:
                        deps[ro] = not (q == "t" and ops[ro]["q"] == "t") or deps.get(ro, False)
                acc[buf] = [me]
                continue
            keep = []
            for rlo, rhi, rw, ro in recs:
                if ro != me and q != "net" and rlo < hi and lo < rhi and (w or rw):
                    deps[ro] = True
                if not (w and rlo >= lo and rhi <= hi and ro != me):
                    keep.append((rlo, rhi, rw, ro))
            keep.append((lo, hi, w, me))
            acc[buf] = keep
    ops.append({"q": q, "fn": fn, "deps": deps, "cost": cost, "token": token, "lat": lat, "boost": boost + P["boost"], "lab": outs[0] if outs else ("out", 0)})
    return me


def gather(P, out, o0, win, w1, lst, l0, l1, sub, scale=None, bias=None, eng="vs"):
    n = 16 * (l1 - l0)

    def fn(g, T, q):
        src = T[win][:, 0:w1].indirect(T[lst][:, l0:l1])
        dst = T[out][:, o0:o0 + n]
        if q == "v":
            if scale is not None:
                return g.vector.tensor_scalar(dst, src, scale, bias, OP.mult, OP.add)
            if sub:
                return g.vector.tensor_scalar(dst, src, sub, None, OP.subtract)
            return g.vector.tensor_copy(dst, src)
        if scale is not None:
            return g.scalar.activation(dst, src, AF.Identity, bias=bias, scale=scale)
        if sub:
            return g.scalar.activation(dst, src, AF.Identity, bias=-sub)
        return g.scalar.activation(dst, src, AF.Copy)
    return add(P, eng, fn, [(out, o0, o0 + n)], [(win, 0, w1), (lst, l0, l1)], 60 + GAT * n)


def shift(P, out, o0, src, s0, n, c, eng="vs"):
    def fn(g, T, q):
        d, s = T[out][:, o0:o0 + n], T[src][:, s0:s0 + n]
        if q == "v":
            return g.vector.tensor_scalar(d, s, c, None, OP.add)
        return g.scalar.activation(d, s, AF.Identity, bias=c)
    return add(P, eng, fn, [(out, o0, o0 + n)], [(src, s0, s0 + n)], 30 + max(64, n) * CYC)


def ts(P, out, o0, src, s0, n, a, b, op0, op1=None, half=False):
    def fn(g, T, q):
        x = T[a[0]][:, a[1]:a[1] + 1] if isinstance(a, tuple) else a
        y = T[b[0]][:, b[1]:b[1] + 1] if isinstance(b, tuple) else b
        d, s = T[out][:, o0:o0 + n], T[src][:, s0:s0 + n]
        if op1 is None:
            return g.vector.tensor_scalar(d, s, x, None, op0)
        return g.vector.tensor_scalar(d, s, x, y, op0, op1)
    ins = [(src, s0, s0 + n)] + [(c[0], c[1], c[1] + 1) for c in (a, b) if isinstance(c, tuple)]
    return add(P, "v", fn, [(out, o0, o0 + n)], ins, 30 + max(64, n * (0.5 if half else 1)) * CYC)


def tt(P, out, o0, x, x0, y, y0, n, op, boost=0.0):
    def fn(g, T, q):
        return g.vector.tensor_tensor(T[out][:, o0:o0 + n], T[x][:, x0:x0 + n], T[y][:, y0:y0 + n], op)
    two = 1 if bank(x) or bank(y) else 2
    return add(P, "v", fn, [(out, o0, o0 + n)], [(x, x0, x0 + n), (y, y0, y0 + n)], 30 + max(64, n * two) * CYC, boost=boost)


def cp(P, out, o0, src, s0, n, f=1):
    def fn(g, T, q):
        return g.vector.tensor_copy(T[out][:, o0:o0 + n], T[src][:, s0:s0 + n])
    return add(P, "v", fn, [(out, o0, o0 + n)], [(src, s0, s0 + n)], 30 + max(64, n * f) * CYC)


def scatter(P, win, w1, lst, n, src, s0, l0=0):
    def fn(g, T, q):
        return g.vector.tensor_copy(T[win][:, 0:w1].indirect(T[lst][:, l0:l0 + n // 16]), T[src][:, s0:s0 + n])
    return add(P, "v", fn, [(win, 0, w1)], [(lst, l0, l0 + n // 16), (src, s0, s0 + n)], 60 + SCA * n)


def mset(P, out, lo, hi, c):
    def fn(g, T, q):
        return g.vector.memset(T[out][:, lo:hi], c)
    return add(P, "v", fn, [(out, lo, hi)], [], 30 + max(64, (hi - lo) * (0.5 if _S[out][1] == BF else 1)) * CYC)


def mm(P, bk, b0, n, terms):
    def fn(g, T, q):
        last = None
        for con, c0, rhs, r0, r1, st, sta, sto in terms:
            last = g.tensor.matmul(T[bk][:, b0:b0 + n], T[con][:, c0:c0 + 128], T[rhs][:, r0:r1:st] if st > 1 else T[rhs][:, r0:r1], sta, sto)
        return last
    ins = {}
    for con, c0, rhs, r0, r1, st, sta, sto in terms:
        ins[(con, c0 // 128)] = (con, c0, c0 + 128)
        lo, hi = ins.get(rhs, (rhs, r0, r1))[1:]
        ins[rhs] = (rhs, min(lo, r0), max(hi, r1))
    return add(P, "t", fn, [(bk, b0, b0 + n)], list(ins.values()), 20 + len(terms) * max(64, n) * PEC)


def slots16(con, rhs, n, start=True, stop=True, r0=0, step=0):
    return [(con, 128 * i * step, rhs, r0 + i, r0 + 16 * n, 16, start and i == 0, stop and i == 15) for i in range(16)]


def dma(P, q, fn, outs, ins):
    k = P["nd"]
    P["nd"] += 1
    return add(P, q, fn, outs, ins, 60.0, token=("d%d" % k, 16), lat=DMA)


def gop(P, fn, outs, ins, n):
    return add(P, "g", lambda g, T, q: fn(g, T), outs, ins, 170 + 2.1 * n, after=(P["s0"],) if n > 128 else ())


def engine_sets(topo, core, dsts):
    eng = topo.engines(core, dsts[0])
    pool = {True: eng[0::2], False: eng[1::2]}
    out = []
    for d in dsts:
        p = pool[topo.die(d) != topo.die(core)]
        out.append(p[:4])
        del p[:4]
    return out


CTX = {}


def exchange(P, step, buf, wide):
    w = 256 if wide else 128
    lst, snd = "SH" if wide else "shl", "SNDh" if buf == "VF" else "SND"
    cols = 3 * w // 16
    for h in range(2):
        gather(P, snd, h * 8 * cols, buf, NV, lst, h * cols // 2, (h + 1) * cols // 2, 0.0)

    def fn(g, T, q):
        topo, core, rank = CTX["topo"], CTX["core"], CTX["rank"]
        dsts = [T.cores[(rank + d) % N] for d in range(1, N)]
        tr = []
        for d, (dst, es) in enumerate(zip(dsts, engine_sets(topo, core, dsts))):
            ad = topo.addr(dst)
            tr.append(RemoteDMATransfer(dst_ids=[DstId(rid=ad[0], pnc=ad[1])], dma_engine_mask=sum(1 << e for e in es), remote_sem=T.sem["arr%d" % step],
                                        src=T[snd][:, d * w:d * w + w], dst=T[buf][:, NV + d * 256:NV + d * 256 + w]))
        g.remote_dma_fused(tr, local_sem=T.sem["snd%d" % step])
        return None
    P["s%d" % step] = add(P, "g", fn, [], [(snd, 0, 3 * w)], 1000.0, token=("snd%d" % step, 12), lat=500.0)
    add(P, "net", None, [(buf, NV + d * 256, NV + d * 256 + w) for d in range(3)], [], NET, token=("arr%d" % step, 12), after=(P["s%d" % step],))


def next_gb(P):
    P["gb"] += 1
    return "gb%d" % (P["gb"] % NGB)


def clip(P, win, out, C, last):
    c0, k = 0, 0
    while c0 < C:
        n = min(PIECE, C - 256 - c0) if c0 < C - 256 else 64
        gb, bk = next_gb(P), "p%d" % (k % 4)
        gather(P, gb, 0, win, W, "Lu", c0, c0 + n, M, eng="s" if last and c0 >= ONLY_S[P["r"]] else "vs")
        mm(P, bk, 0, n, slots16("Id8", gb, n, True, False) + [("dneg", 0, "ONE", 0, n, 1, False, False), ("dmag", 0, "ONE", 0, n, 1, False, True)])
        tt(P, out, c0, win, c0, bk, 0, n, OP.min, BOOST)
        if last:
            P["boost"] = BOOST
            shift(P, "VF", c0, out, c0, n, -M)
            P["boost"] = 0.0
        c0, k = c0 + n, k + 1


def blocks(NC):
    out, c = [], 0
    while c < NC:
        n = 512 if NC - c > 512 else 256
        out.append((c, n))
        c += n
    return out


def relu(P, out, o0, src, s0, n, bias):
    def fn(g, T, q):
        d, s = T[out][:, o0:o0 + n], T[src][:, s0:s0 + n]
        if q == "v":
            return g.vector.tensor_scalar(d, s, bias, 0.0, OP.add, OP.max)
        return g.scalar.activation(d, s, AF.Relu, bias=bias)
    return add(P, "vs", fn, [(out, o0, o0 + n)], [(src, s0, s0 + n)], 30 + n * CYC)


def pointers(P, NC, final):
    for c0, n in blocks(NC):
        relu(P, "em", c0, "E", c0, n, float(K + 1 - NONE))
        mm(P, "p7", 0, n, [("TRI", 0, "em", c0, c0 + n, 1, True, True)])
        relu(P, "fe", c0, "p7", 0, n, 0.0)
        if final:
            shift(P, "fp", c0, "E", c0, n, float(K))
    for b, (c0, n) in enumerate(blocks(NC)):
        Q, Y, G = "p%d" % (b % 2), "p%d" % (2 + b % 2), "p%d" % (4 + b % 2)
        if not final:
            mm(P, Q, 0, n, [("dneg", 0, "ONE", 0, n, 1, True, False)])
        for s0 in range(0, n, SUB):
            gb = next_gb(P)
            gather(P, gb, 0, "VF", W, "Lu", c0 + s0, c0 + s0 + SUB, 0.0)
            if not final:
                mm(P, Q, s0, SUB, slots16("Id8", gb, SUB, False, False))
            mm(P, Y, s0, SUB, slots16("Dm", gb, SUB, True, True, 0, 1))
        ts(P, "fl", c0, Y, 0, n, 0.0, None, OP.is_lt)
        mm(P, G, 0, n, [("TRI", 0, "fl", c0, c0 + n, 1, True, False), ("BD", 0, "fe", c0, c0 + n, 1, False, True)])
        if not final:
            mm(P, Q, 0, n, [("BO32", 0, "fl", c0, c0 + n, 1, False, False)])
        relu(P, G, 0, G, 0, n, -1.0)
        tt(P, "prod", c0, "E", c0, G, 0, n, OP.mult)
        mm(P, "p6", 0, n // 16, slots16("R16", "prod", n // 16, True, True, c0, 1))
        ts(P, "tl", c0 // 16, "p6", 0, n // 16, float(K), None, OP.add)
        if not final:
            gather(P, "xp", c0, "VF", W, "tl", c0 // 16, (c0 + n) // 16, 0.0, eng="s")
            ts(P, "xi", c0, "xp", c0, n, 0.0, 256.0, OP.is_lt, OP.mult, half=True)
            mm(P, Q, 0, n, [("Id8", 0, "xp", c0, c0 + n, 1, False, False), ("Id8", 0, "xi", c0, c0 + n, 1, False, False), ("dmag", 0, "ONE", 0, n, 1, False, True)])
            tt(P, "B", c0, "A", c0, Q, 0, n, OP.min)
        ptr = "B" if final else "fp"

        def ffp(g, T, q, c0=c0, n=n):
            return g.vector.tensor_tensor(T[ptr][:, c0:c0 + n], T.H[:, 0:W].indirect(T.tl[:, c0 // 16:(c0 + n) // 16]), T.fe[:, c0:c0 + n], OP.mult)
        add(P, "v", ffp, [(ptr, c0, c0 + n)], [("H", 0, W), ("tl", c0 // 16, (c0 + n) // 16), ("fe", c0, c0 + n)], 60 + GAT * n)
        if not final:
            tt(P, "E", c0, "E", c0, "fp", c0, n, OP.add)
            ts(P, "Lu", c0, "E", c0, n, float(K), None, OP.add)
        else:
            tt(P, "fp", c0, "fp", c0, "B", c0, n, OP.add)
            dma(P, "y", lambda g, T, q, c0=c0, n=n: g.sync.dma_start(T.ye[:, c0:c0 + n], T.fp[:, c0:c0 + n]), [], [("fp", c0, c0 + n)])


def split(P, r):
    final = r == RO - 1
    h0 = L + CAP * r

    def fpre(g, T, q):
        return g.scalar.activation(T.SLW[:, 0:256], T.CI[:, 0:256], AF.Identity, bias=T.pc[:, r:r + 1])
    add(P, "s", fpre, [("SLW", 0, 256)], [("CI", 0, 256), ("pc", r, r + 1)], 300)
    P["boost"] = BOOST
    for m0, m1 in PARTS:
        n = m1 - m0
        terms = [("Rm", 128 * i, "VF", 16 * m0 + i, 16 * m1, 16, i == 0, i == 15 and r == 0) for i in range(16)]
        if r:
            terms.append(("dsp", 0, "spl", m0, m1, 1, False, True))
        mm(P, "p6", m0, n, terms)
        ts(P, "cand", m0, "p6", m0, n, ("thf", 0), None, OP.is_ge)
        mm(P, "p7", m0, n, [("BD", 0, "cand", m0, m1, 1, True, True)])
        mm(P, "p7", 128 + m0, n, [("PXl", 0, "cand", m0, m1, 1, True, True)])

        def fscan(g, T, q, m0=m0, m1=m1):
            first = T.SC[:, m0 - 1:m0] if m0 else T.ini[:, 0:1]
            return g.vector.tensor_tensor_scan(T.SC[:, m0:m1], T.p7[:, m0:m1], T.d16[:, m0:m1], first, OP.add, OP.add)
        add(P, "v", fscan, [("SC", m0, m1)], [("p7", m0, m1), ("d16", m0, m1), ("SC", m0 - 1, m0) if m0 else ("ini", 0, 1)], 110)
        tt(P, "pd", m0, "SC", m0, "p7", 128 + m0, n, OP.add)
        tt(P, "tt", m0, "pd", m0, "cand", m0, n, OP.mult)
        tt(P, "of", m0, "tt", m0, "DU", m0, n, OP.add)
        cp(P, "ofu", m0, "of", m0, n)
        scatter(P, "SLW", 2560, "ofu", 16 * n, "CI", 16 * m0, m0)
        if not final:
            ts(P, "val" if r else "spl", m0, "of", m0, n, 255.5, None, OP.is_le)
            if r:
                tt(P, "spl", m0, "spl", m0, "val", m0, n, OP.add)
    P["boost"] = 0.0
    mm(P, "p5", 0, 16, slots16("Ls", "SLW", 16, True, True, 0, 1))
    cp(P, "SL", 0, "p5", 0, 16)
    scatter(P, "H", NV, "SL", 256, "HJ", 256 * r)
    if final:
        mset(P, "H", K, K + 1, 0.0)
    gather(P, "EO", 0, "E", NV, "SL", 0, 16, 0.0)
    gather(P, "XS", 0, "VF", NV, "SL", 0, 16, 0.0, 0.5, 0.25)
    shift(P, "NB", 0, "XS", 0, 256, M)
    shift(P, "FN", 0, "NB", 0, 256, -M - 256.0)
    scatter(P, "VF", NV, "SL", 256, "FN", 0)
    shift(P, "VF", h0, "NB", 0, 256, -M)
    if not final:
        def fhg(g, T, q):
            return g.vector.tensor_scalar(T.HG[:, 0:384], T.H[:, 0:NV].indirect(T.shl[:, 0:24]), 0.0625, None, OP.mult)
        add(P, "v", fhg, [("HG", 0, 384)], [("H", 0, NV), ("shl", 0, 24)], 60 + GAT * 384)
        mm(P, "p4", 0, 24, slots16("R16", "HG", 24, True, True, 0, 1))
        for d in range(3):
            ts(P, "SH", 16 * d + 8, "p4", 8 * d, 8, float(NONE), float(K), OP.add, OP.min)
    exchange(P, 3 * r + 3, "VF", not final)
    ts(P, "EL", 0, "EO", 0, 256, float(K), None, OP.add)
    shift(P, "TO", 0, "EO", 0, 256, float(K - NONE))
    for s0 in range(0, 256, 64):
        gb = next_gb(P)
        gather(P, gb, 0, "A", W, "EL", s0, s0 + 64, M)
        mm(P, "p3", s0, 64, slots16("Wt", gb, 64, True, True, 0, 1))
    ts(P, "BH", 0, "p3", 0, 256, ("thr", 0), None, OP.is_ge)
    tt(P, "TB", 0, "TO", 0, "BH", 0, 256, OP.mult)
    tt(P, "ES", 0, "EO", 0, "TB", 0, 256, OP.subtract)
    scatter(P, "E", NV, "SL", 256, "ES", 0)
    shift(P, "E", h0, "TB", 0, 256, float(NONE - K))
    for c0, n in ((0, 128), (128, 128), (256, 256)) + tuple(x for x in blocks(h0 + CAP) if x[0]):
        ts(P, "Lu", c0, "E", c0, n, float(K), None, OP.add)
    scatter(P, "A", NV, "SL", 256, "NB", 0)
    shift(P, "A", h0, "NB", 0, 256, 0.0)
    if final:
        for c0 in (0, 1024):
            shift(P, "YV", c0, "A", c0, 1024, -M)
            dma(P, "y", lambda g, T, q, c0=c0: g.sync.dma_start(T.yv[:, c0:c0 + 1024], T.YV[:, c0:c0 + 1024]), [], [("YV", c0, c0 + 1024)])


def setup(P):
    dma(P, "y", lambda g, T, q: g.sync.dma_start(T.shi[:], T.sh[:]), [("shi", 0, 24)], [])
    for c in (0, 640):
        dma(P, "y" if c else "sd", lambda g, T, q, c=c: (g.sync if c else g.scalar).dma_start(T.v016[:, c:c + 640], T.v0[:, c:c + 640]), [("v016", c, c + 640)], [])
    for k, c in enumerate(range(0, L, 256)):
        dma(P, "y" if k % 2 else "sd", lambda g, T, q, c=c, k=k: (g.sync if k % 2 else g.scalar).dma_start(T.e32[:, c:c + 256], T.e[:, c:c + 256]), [("e32", c, c + 256)], [])
    dma(P, "y", lambda g, T, q: g.sync.dma_start(T.thi[:], T.th[:]), [("thi", 0, 1)], [])
    cp(P, "shl", 0, "shi", 0, 24)
    mset(P, "A", L, NV, M)
    for c in (0, 640):
        shift(P, "A", c, "v016", c, 640, M)
    mset(P, "ONE", 0, 2048, 1.0)
    exchange(P, 0, "A", False)
    for d in range(3):
        mset(P, "A", NV + 256 * d + 128, NV + 256 * d + 256, M)
    mset(P, "A", NONE, W, M)
    for c in range(0, L, 256):
        cp(P, "Lu", c, "e32", c, 256)
    i1 = dict(allow_small_or_imprecise_dtypes=True)
    gop(P, lambda g, T: g.iota(T.ki[:], [[1, 1]], 0, 1), [("ki", 0, 1)], [], 1)
    gop(P, lambda g, T: g.affine_select(T.Id[:], T.ONE[:, 0:128], [[-1, 128]], OP.is_equal, 0.0, 0, 1), [("Id", 0, 128)], [("ONE", 0, 128)], 128)
    for nm, c in (("Id8", 0.125), ("dneg", -0.4375), ("dmag", M), ("dsp", -8192.0)):
        ts(P, nm, 0, "Id", 0, 128, c, None, OP.mult, half=True)
    for c, hi in (("CH", 1), ("CL", 0)):
        gop(P, lambda g, T, c=c, hi=hi: g.iota(T[c][:], [[hi, 80], [1 - hi, 16]], 0, 0, **i1), [(c, 0, L)], [], L)
    gop(P, lambda g, T: g.iota(T.B[:, L:NV], [[0, NV - L]], int(M), 0, **i1), [("B", L, NV)], [], NV - L)
    for d in range(3):
        gop(P, lambda g, T, d=d: g.iota(T.B[:, NV + 256 * d + 128:NV + 256 * d + 256], [[0, 128]], int(M), 0, **i1), [("B", NV + 256 * d + 128, NV + 256 * d + 256)], [], 128)
    gop(P, lambda g, T: g.iota(T.B[:, NONE:W], [[0, 1]], int(M), 0, **i1), [("B", NONE, W)], [], 1)
    gop(P, lambda g, T: g.iota(T.DU0[:], [[16, 80]], L, 0, **i1), [("DU0", 0, 80)], [], 80)
    gop(P, lambda g, T: g.iota(T.d16[:], [[0, 80]], -16, 0, **i1), [("d16", 0, 80)], [], 80)
    a16, up, dn, blk = [[-1, 16], [0, 8], [1, 16]], [[0, 16], [-16, 8], [0, 16]], [[0, 16], [16, 8], [0, 16]], [("BD", 0, 2048)]
    gop(P, lambda g, T: g.affine_select(T.BD[:], T.ONE[:], up, OP.is_ge, 0.0, 0, 1), blk, [("ONE", 0, 2048)], 2048)
    gop(P, lambda g, T: g.affine_select(T.BD[:], T.BD[:], dn, OP.is_ge, 0.0, 15, -1), blk, blk, 2048)
    gop(P, lambda g, T: g.affine_select(T.Rm[:], T.BD[:], a16, OP.is_equal, 0.0, 0, 0), [("Rm", 0, 2048)], blk, 2048)
    gop(P, lambda g, T: g.affine_select(T.U1[:], T.BD[:, 0:128], [[-1, 128]], OP.is_gt, 0.0, 0, 1), [("U1", 0, 128)], [("BD", 0, 128)], 128)
    ts(P, "PXl", 0, "U1", 0, 128, -1.0, None, OP.mult, half=True)
    gop(P, lambda g, T: g.iota(T.HJ[:], [[1, 768]], L - NONE, 0, **i1), [("HJ", 0, 768)], [], 768)
    gop(P, lambda g, T: g.iota(T.H[:, 0:NV], [[0, NV]], 0, 0, **i1), [("H", 0, NV)], [], NV)
    gop(P, lambda g, T: g.iota(T.H[:, NV:NONE], [[1, 768]], NV + 128 - NONE, 0, **i1), [("H", NV, NONE)], [], 768)
    gop(P, lambda g, T: g.iota(T.H[:, NONE:W], [[0, 1]], 0, 0, **i1), [("H", NONE, W)], [], 1)
    gop(P, lambda g, T: g.affine_select(T.Dm[:], T.ONE[:], [[-1, 16], [-16, 8], [0, 16]], OP.is_equal, 0.0, 0, 1), [("Dm", 0, 2048)], [("ONE", 0, 2048)], 2048)
    gop(P, lambda g, T: g.affine_select(T.Dm[:], T.Dm[:], a16, OP.is_equal, 0.0, 0, 0), [("Dm", 0, 2048)], [("Dm", 0, 2048)], 2048)
    wt = [("Wt", 0, 2048)]
    gop(P, lambda g, T: g.affine_select(T.Wt[:], T.BD[:], a16, OP.is_ge, -1.0, -1, 0), wt, blk, 2048)
    gop(P, lambda g, T: g.affine_select(T.Wt[:], T.Wt[:], up, OP.is_ge, 0.0, 0, 1), wt, wt, 2048)
    gop(P, lambda g, T: g.affine_select(T.Wt[:], T.Wt[:], dn, OP.is_ge, 0.0, 15, -1), wt, wt, 2048)
    gop(P, lambda g, T: g.affine_select(T.U2[:], T.BD[:, 0:128], [[1, 128]], OP.is_gt, 0.0, 0, -1), [("U2", 0, 128)], [("BD", 0, 128)], 128)
    add(P, "v", lambda g, T, q: g.vector.tensor_scalar(T.ka[:], T.ki[:], 15, None, OP.bitwise_and), [("ka", 0, 1)], [("ki", 0, 1)], 100)
    cp(P, "km", 0, "ka", 0, 1)
    cp(P, "thf", 0, "thi", 0, 1)
    ts(P, "thr", 0, "km", 0, 1, 0.0, None, OP.is_equal)
    ts(P, "c1", 0, "km", 0, 1, 0.0, 16.0, OP.is_equal, OP.mult)
    ts(P, "c2", 0, "km", 0, 1, 8.0, None, OP.is_equal)
    tt(P, "cc", 0, "c1", 0, "c2", 0, 1, OP.add)
    ts(P, "mhi", 0, "km", 0, 1, 8.0, None, OP.is_lt)
    ts(P, "mlo", 0, "km", 0, 1, 8.0, None, OP.is_ge)
    for r in range(RO):
        ts(P, "pc", r, "mhi", 0, 1, float(80 + 16 * r), None, OP.mult)
    ts(P, "ini", 0, "km", 0, 1, -1.0, float(15 - L), OP.mult, OP.add)
    ts(P, "DU", 0, "DU0", 0, 80, ("km", 0), None, OP.add)
    for nm, c in (("Ihi", "mhi"), ("Ilo", "mlo")):
        ts(P, nm, 0, "Id", 0, 128, (c, 0), None, OP.mult, half=True)
    for k, c0 in enumerate((0, 512, 1024)):
        n, bk = min(512, L - c0), "p%d" % (5 + k)
        mm(P, bk, 0, n, [("Ihi", 0, "CH", c0, c0 + n, 1, True, False), ("Ilo", 0, "CL", c0, c0 + n, 1, False, True)])
        shift(P, "CI", c0, bk, 0, n, 0.0)
    ts(P, "BO32", 0, "BD", 0, 128, 32.0, None, OP.mult, half=True)
    tt(P, "TRI", 0, "Id", 0, "U2", 0, 128, OP.subtract)
    ts(P, "Ls", 0, "Rm", 0, 2048, ("cc", 0), None, OP.mult, half=True)
    cp(P, "R16", 0, "Rm", 0, 2048, 0.5)
    mset(P, "VF", L, NV, 0.0)
    mset(P, "VF", NONE, W, 0.0)
    mset(P, "E", L, NV, float(NONE - K))
    ts(P, "E", 0, "e32", 0, L, float(-K), None, OP.add)
    for d in range(3):
        cp(P, "SH", 16 * d, "shi", 8 * d, 8)


def program():
    P = {"ops": [], "acc": {}, "nd": 0, "gb": 0, "boost": 0.0}
    setup(P)
    for r in range(RO):
        C = L + CAP * r
        P["r"] = r
        if r == 0:
            clip(P, "A", "B", C, False)
        exchange(P, 3 * r + 1, "B", r > 0)
        clip(P, "B", "A", C, True)
        exchange(P, 3 * r + 2, "A", r > 0)
        split(P, r)
        pointers(P, C + CAP, r == RO - 1)
    return P


def plan(P):
    ops = P["ops"]
    n = len(ops)
    users = [[] for _ in range(n)]
    for i, o in enumerate(ops):
        for d in o["deps"]:
            users[d].append(i)
    prio = [0.0] * n
    for i in range(n - 1, -1, -1):
        prio[i] = ops[i]["cost"] + ops[i]["lat"] + max([prio[u] + WAKE for u in users[i]] or [0.0])
    prio = [p + o["boost"] for p, o in zip(prio, ops)]
    queues = ("v", "s", "t", "g", "y", "net")
    free = {q: 0.0 for q in queues}
    ready = {q: {} for q in queues + ("vs",)}
    left = [len(o["deps"]) for o in ops]
    end, at, run, order = [0.0] * n, [0.0] * n, [None] * n, []

    def push(i):
        q = ops[i]["q"]
        ready["s" if q == "sd" else q][i] = None
    for i in range(n):
        if not left[i]:
            push(i)
    while len(order) < n:
        best = None
        for q in queues:
            for pool in ((q, "vs") if q in "vs" else (q,)):
                for i in ready[pool]:
                    st = 0.0 if q == "net" else free[q]
                    for d, hard in ops[i]["deps"].items():
                        if hard:
                            st = max(st, end[d] + (OWN if run[d] == q else WAKE))
                    k = (int(st / 150.0), -prio[i], st)
                    if best is None or k < best[0]:
                        best = (k, st, i, q, pool)
        _, st, i, q, pool = best
        del ready[pool][i]
        run[i], at[i] = q, st
        if q != "net":
            free[q] = st + ops[i]["cost"]
        end[i] = st + ops[i]["cost"] + ops[i]["lat"]
        order.append(i)
        for u in users[i]:
            left[u] -= 1
            if not left[u]:
                push(u)
    return order, run, at, end


CACHE = {}


def compiled():
    if "x" not in CACHE:
        P = program()
        CACHE["x"] = (P,) + plan(P)
    return CACHE["x"]


def rank_program(g, core, T, topo):
    rank = T.rank_of(core)
    if rank is None:
        return
    CTX.update({"topo": topo, "core": core, "rank": rank})
    P, order, run, at, end = compiled()
    ops = P["ops"]
    queue = {"v": g.vector, "s": g.scalar, "t": g.tensor, "g": g, "y": g.sync}
    known = {q: {} for q in queue}
    count, tok, clock, total = {q: 0 for q in queue}, {}, {}, {}
    for i in order:
        o, q = ops[i], run[i]
        if q == "net":
            tok[i] = o["token"]
            clock[i] = {tok[i][0]: tok[i][1]}
        else:
            kn = known[q]
            for d in sorted((d for d, hard in o["deps"].items() if hard), key=lambda d: -at[d]):
                s, v = tok[d]
                if kn.get(s, 0) < v:
                    queue[q].wait_ge(T.sem[s], v)
                    for s2, v2 in clock[d].items():
                        kn[s2] = max(kn.get(s2, 0), v2)
            ins = o["fn"](g, T, q)
            if o["token"] is not None:
                tok[i] = o["token"]
            else:
                count[q] += 1
                tok[i] = ("q" + q, count[q])
            if ins is not None:
                ins.then_inc(T.sem[tok[i][0]], 1 if o["token"] is None else tok[i][1])
            clock[i] = dict(kn)
            clock[i][tok[i][0]] = tok[i][1]
        total[tok[i][0]] = tok[i][1]
    for s, v in total.items():
        if known["g"].get(s, 0) < v:
            g.wait_ge(T.sem[s], v)
